import numpy as np
import ml_dtypes


def mxq(x, axis, fmt="e4m3"):
    dtype, down = {"e4m3": (ml_dtypes.float8_e4m3fn, 7), "e5m2": (ml_dtypes.float8_e5m2, 14)}[fmt]
    v = np.moveaxis(np.asarray(x, np.float32).astype(ml_dtypes.bfloat16).astype(np.float64), axis, -1)
    blocks = v.reshape(v.shape[:-1] + (-1, 32))
    amax = np.abs(blocks).max(-1, keepdims=True)
    byte = np.maximum(np.where(amax > 0, np.frexp(amax)[1] - 1 + 127, 0) - down, 1)
    scale = np.exp2(byte - 127.0)
    codes = (blocks / scale).astype(np.float32).astype(dtype).astype(np.float64)
    return np.moveaxis((codes * scale).reshape(v.shape), -1, axis)


WIDE = False


def mx_kscale(k):
    if not WIDE:
        return np.ones(k)
    levels = np.array([10, -10, 5, -5, 0])
    if k % 512:
        return np.exp2(np.random.permutation(np.resize(levels, k // 32))).repeat(32)
    a = np.empty((k // 512, 16))
    for p in range(k // 512):
        a[p, :8] = np.random.permutation(np.resize(levels, 8))
        for g in range(8):
            far = levels[np.abs(levels - a[p, g]) >= 10]
            a[p, g + 8] = far[np.random.randint(len(far))]
    return np.exp2(a.ravel()).repeat(32)


def f64(x):
    return np.asarray(x).astype(np.float64)


def striped(idx):
    return np.tile(idx.reshape(-1, 16).T, (8, 1)).astype(np.uint16)


def unstriped(offs):
    return offs[:16].T.reshape(-1).astype(np.int64)


def striped8(idx):
    return np.concatenate([x.reshape(-1, 16).T for x in idx]).astype(np.uint16)


def runs(offs, k):
    lists = np.stack([offs[16 * r : 16 * r + 16].T.reshape(-1) for r in range(8)]).astype(np.int64)
    return lists[np.arange(k) % 512 // 64]


def pack_weight(w):
    k, n = w.shape
    w = f64(np.asarray(w, np.float32).astype(ml_dtypes.bfloat16)).reshape(k // 32, 32, n)
    amax = np.abs(w).max(1)
    byte = np.clip(np.where(amax > 0, np.frexp(amax)[1] - 1 + 127 - 7, 1), 1, 254)
    scaled = (w * np.exp2(127.0 - byte)[:, None, :]).reshape(k, n).astype(np.float32)
    words = np.ascontiguousarray(scaled.reshape(k // 512, 128, 4, n).transpose(0, 1, 3, 2)).astype(ml_dtypes.float8_e4m3fn).view(np.uint8)
    return words, np.ascontiguousarray(byte.astype(np.uint8).reshape(k // 512, 16, n))


def unpack_weight(words, scales):
    g, p, n, _ = words.shape
    vals = np.ascontiguousarray(words).view(ml_dtypes.float8_e4m3fn).astype(np.float64) * np.repeat(np.exp2(scales.astype(np.float64) - 127.0), 8, axis=1)[..., None]
    return vals.transpose(0, 1, 3, 2).reshape(g * 512, n)


def relu(v):
    return np.maximum(v, 0.0)

def planes(y):
    n, m = y.shape
    v = y.astype(np.float32).astype(ml_dtypes.bfloat16).astype(np.float64).reshape(n // 32, 32, m)
    top = np.abs(v).max(1)
    byte = np.clip(np.where(top > 0, np.frexp(top)[1] - 1 + 127 - 7, 1), 1, 254)
    codes = (v * np.exp2(127.0 - byte)[:, None, :]).reshape(n, m).astype(np.float32).astype(ml_dtypes.float8_e4m3fn).view(np.uint8)
    words = codes.reshape(n // 512, 128, 4, m).transpose(0, 1, 3, 2)
    return np.ascontiguousarray(words), np.ascontiguousarray(byte.astype(np.uint8).reshape(n // 512, 16, m))


K, T, S, V, N, U, H = 512, 2048, 512, 1024, 512, 1024, 512


def setup_inputs():
    n = np.random.standard_normal
    s = mx_kscale(K)[:, None]
    u = mx_kscale(H)
    packed_xT = pack_weight(n((K, T)) * s)
    packed_w3 = pack_weight(n((H, N)) / np.sqrt(H) / u[:, None])
    return {
        "x_words": packed_xT[0],
        "x_scales": packed_xT[1],
        "w1": (n((K, H)) / np.sqrt(K) / s * u).astype(np.float32),
        "mem": (n((H, U)) * u[:, None]).astype(np.float32),
        "w2": (n((H, H)) / np.sqrt(H) / u[:, None] * u).astype(np.float32),
        "w3_words": packed_w3[0],
        "w3_scales": packed_w3[1],
        "offs": striped(np.random.permutation(T)[:S]),
        "slot": striped8(np.stack([np.random.permutation(U)[:S] for _ in range(8)])),
        "rd": striped8(np.random.randint(0, U, (8, S))),
        "put": striped8(np.stack([np.random.permutation(U)[:S] for _ in range(8)])),
        "rd2": striped8(np.stack([np.random.permutation(U) for _ in range(8)])),
    }


def reference(x_words, x_scales, w1, mem, w2, w3_words, w3_scales, offs, slot, rd, put, rd2):
    xq = unpack_weight(x_words, x_scales)[:, unstriped(offs)]
    y = mxq(f64(w1), 0, "e4m3").T @ xq
    pg = f64(mem).copy()
    pg[np.arange(H)[:, None], runs(slot, H)] = y
    z = pg[np.arange(H)[:, None], runs(rd, H)]
    h = relu(mxq(f64(w2), 0, "e4m3").T @ mxq(z, 0, "e4m3"))
    pg2 = pg.copy()
    pg2[np.arange(H)[:, None], runs(put, H)] = h
    z2 = pg2[np.arange(H)[:, None], runs(rd2, H)]
    out_0 = unpack_weight(w3_words, w3_scales).T @ mxq(z2, 0, "e4m3")
    return (out_0,) + planes(out_0)

@@ -1,0 +1,267 @@
+from contextlib import ExitStack
+
+import concourse.mybir as mybir
+
+K, T, S, V, N, U, H = 512, 2048, 512, 1024, 512, 1024, 512
+FLOPS = 2 * K * H * S + 2 * H * H * S + 2 * H * N * V
+
+F32 = mybir.dt.float32
+BF16 = mybir.dt.bfloat16
+I32 = mybir.dt.int32
+U32 = mybir.dt.uint32
+U16 = mybir.dt.uint16
+U8 = mybir.dt.uint8
+FP8X4 = mybir.dt.float8_e4m3fn_x4
+RELU = mybir.ActivationFunctionType.Relu
+
+P = 128
+PACK = 4
+CHUNK = 256
+HALF = 128
+W1_VECTOR_SHARE = 80
+SCALAR_CHUNKS = (0,)
+
+
+def entries(lists, first, count):
+    return lists[:, first // 16 : (first + count) // 16]
+
+
+def deal_weight(engine_copy, grouped, raw, m0, m1):
+    engine_copy(
+        out=grouped[:].rearrange("p t m j -> p m j t")[:, m0:m1],
+        in_=raw[:].rearrange("p j (m t) -> p m j t", t=PACK)[:, m0:m1],
+    )
+
+
+def interleave(engine_copy, out, in_):
+    engine_copy(
+        out=out.rearrange("p (c i t) -> p c t i", i=4, t=PACK),
+        in_=in_.rearrange("p t (c i) -> p c t i", i=4),
+    )
+
+
+def load_scale_rows(nc, plane, rows):
+    for q in range(4):
+        nc.sync.dma_start(
+            out=plane[32 * q : 32 * q + 4, :].bitcast(I32),
+            in_=rows[4 * q : 4 * q + 4, :].bitcast(I32),
+        )
+
+
+def tile_picked_pagerd_relu_po_kernel(
+    tc, x_words, x_scales, w1, mem, w2, w3_words, w3_scales, offs, slot, rd, put, rd2, out_0, out_1, out_2
+):
+    nc = tc.nc
+    with ExitStack() as ctx:
+        keep = ctx.enter_context(tc.tile_pool(name="keep", bufs=1))
+        psum = ctx.enter_context(tc.psum_pool(name="psum", bufs=8))
+
+        def mx_product(out, w_codes, w_scales, t, codes, scales):
+            cols = slice(t * P, (t + 1) * P)
+            nc.tensor.matmul_mx(
+                out=out,
+                lhsT=w_codes[:, cols].bitcast(FP8X4),
+                lhsT_scale=w_scales[:, cols],
+                rhs=codes.bitcast(FP8X4),
+                rhs_scale=scales,
+                start=True,
+                stop=True,
+            )
+
+        offs_list = keep.tile([P, S // 16], U16)
+        slot_list = keep.tile([P, S // 16], U16)
+        rd_list = keep.tile([P, S // 16], U16)
+        put_list = keep.tile([P, S // 16], U16)
+        rd2_list = keep.tile([P, V // 16], U16)
+        x_table = keep.tile([P, T], I32, align_bytes=64)
+        x_scale_table = keep.tile([P, T], U8, align_bytes=64)
+        w1_raw = keep.tile([P, PACK, H], F32)
+        w2_raw = keep.tile([P, PACK, H], F32)
+        w3_table = keep.tile([P, N], I32, align_bytes=64)
+        w3_scale_table = keep.tile([P, N], U8, align_bytes=64)
+        page = [keep.tile([P, U], F32, name="page%d" % t, align_bytes=64) for t in range(PACK)]
+
+        nc.vector.memset(x_scale_table[:].bitcast(I32), 0)
+        nc.vector.memset(w3_scale_table[:].bitcast(I32), 0)
+
+        mem_rows = mem.rearrange("(p t) u -> t p u", t=PACK)
+        nc.sync.dma_start(out=w1_raw[:], in_=w1.rearrange("(p j) c -> p j c", j=PACK))
+        load_scale_rows(nc, x_scale_table, x_scales[0])
+        nc.sync.dma_start(offs_list[:], offs)
+        nc.sync.dma_start(out=x_table[:], in_=x_words[0].rearrange("p n r -> p (n r)").bitcast(I32))
+        nc.sync.dma_start(slot_list[:], slot)
+        nc.sync.dma_start(out=page[0][:], in_=mem_rows[0])
+        nc.sync.dma_start(out=page[1][:], in_=mem_rows[1])
+        nc.sync.dma_start(rd_list[:], rd)
+        nc.sync.dma_start(out=page[2][:], in_=mem_rows[2])
+        nc.sync.dma_start(out=page[3][:], in_=mem_rows[3])
+        nc.sync.dma_start(out=w2_raw[:], in_=w2.rearrange("(p j) c -> p j c", j=PACK))
+        nc.sync.dma_start(put_list[:], put)
+        nc.sync.dma_start(out=w3_table[:], in_=w3_words[0].rearrange("p n r -> p (n r)").bitcast(I32))
+        load_scale_rows(nc, w3_scale_table, w3_scales[0])
+        nc.sync.dma_start(rd2_list[:], rd2)
+
+        w1_grouped = keep.tile([P, PACK, P, PACK], BF16, align_bytes=64)
+        deal_weight(nc.vector.tensor_copy, w1_grouped, w1_raw, 0, W1_VECTOR_SHARE)
+        deal_weight(nc.scalar.copy, w1_grouped, w1_raw, W1_VECTOR_SHARE, P)
+        x_bytes = keep.tile([P, S], U8, align_bytes=64)
+        nc.vector.tensor_copy(out=x_bytes[:], in_=x_scale_table[:].indirect(offs_list[:]))
+        w1_codes = keep.tile([P, H], U32, align_bytes=64)
+        w1_bytes = keep.tile([P, H], U8, align_bytes=64)
+        nc.vector.quantize_mx(
+            out=w1_codes[:].bitcast(FP8X4),
+            scales=w1_bytes[:],
+            in_=w1_grouped[:].rearrange("p t m j -> p (t m j)"),
+        )
+
+        x_codes = keep.tile([P, S], U32, align_bytes=64)
+        for c0 in range(0, S, CHUNK):
+            nc.vector.tensor_copy(
+                out=x_codes[:, c0 : c0 + CHUNK],
+                in_=x_table[:].bitcast(U32).indirect(entries(offs_list, c0, CHUNK)),
+            )
+
+        y_sb = [keep.tile([P, S], F32, name="y%d" % t, tag="y%d" % t, align_bytes=64) for t in range(PACK)]
+        for t in range(PACK):
+            width = CHUNK if t == 0 else S
+            for c0 in range(0, S, width):
+                cols = slice(c0, c0 + width)
+                bank = psum.tile([P, S], F32, tag="bank")
+                mx_product(bank[:, :width], w1_codes, w1_bytes, t, x_codes[:, cols], x_bytes[:, cols])
+                nc.scalar.copy(out=y_sb[t][:, cols], in_=bank[:, :width])
+                nc.vector.tensor_copy(out=page[t][:].indirect(entries(slot_list, c0, width)), in_=y_sb[t][:, cols])
+
+        w2_grouped = keep.tile([P, PACK, P, PACK], BF16, align_bytes=64)
+        deal_weight(nc.scalar.copy, w2_grouped, w2_raw, 0, P)
+        w2_codes = keep.tile([P, H], U32, align_bytes=64)
+        w2_bytes = keep.tile([P, H], U8, align_bytes=64)
+
+        def read_page(out, t, lists, c0):
+            nc.vector.tensor_copy(
+                out=out[:, t * CHUNK : (t + 1) * CHUNK],
+                in_=page[t][:].indirect(entries(lists, c0, CHUNK)),
+            )
+
+        z_first = keep.tile([P, PACK * CHUNK], BF16, align_bytes=64)
+        z_shared = keep.tile([P, 6 * CHUNK], BF16, tag="y3", align_bytes=64)
+        z_second = z_shared[:, : PACK * CHUNK]
+        z_first_grouped = z_shared[:, 2 * CHUNK :]
+        z_codes = keep.tile([P, S], U32, align_bytes=64)
+        z_bytes = keep.tile([P, S], U8, align_bytes=64)
+
+        def second_layer(t, c, tag):
+            cols = slice(c * CHUNK, (c + 1) * CHUNK)
+            bank = psum.tile([P, S], F32, tag="bank")
+            mx_product(bank[:, :CHUNK], w2_codes, w2_bytes, t, z_codes[:, cols], z_bytes[:, cols])
+            h = keep.tile([P, CHUNK], F32, name="h", tag=tag, align_bytes=64)
+            nc.scalar.activation(out=h[:], in_=bank[:, :CHUNK], func=RELU)
+            nc.vector.tensor_copy(out=page[t][:].indirect(entries(put_list, c * CHUNK, CHUNK)), in_=h[:])
+
+        for t in range(PACK):
+            read_page(z_first, t, rd_list, 0)
+        interleave(nc.scalar.copy, z_first_grouped, z_first[:].rearrange("p (t n) -> p t n", t=PACK))
+        for t in range(2):
+            read_page(z_second, t, rd_list, CHUNK)
+        nc.vector.quantize_mx(
+            out=w2_codes[:].bitcast(FP8X4),
+            scales=w2_bytes[:],
+            in_=w2_grouped[:].rearrange("p t m j -> p (t m j)"),
+        )
+        nc.vector.quantize_mx(out=z_codes[:, :CHUNK].bitcast(FP8X4), scales=z_bytes[:, :CHUNK], in_=z_first_grouped)
+        for t in range(2, PACK):
+            read_page(z_second, t, rd_list, CHUNK)
+        second_layer(0, 0, "h00")
+        z_second_grouped = keep.tile([P, PACK * CHUNK], BF16, tag="h00", align_bytes=64)
+        interleave(nc.scalar.copy, z_second_grouped[:], z_second.rearrange("p (t n) -> p t n", t=PACK))
+        second_layer(1, 0, "h10")
+        second_layer(2, 0, "h20")
+        nc.vector.quantize_mx(out=z_codes[:, CHUNK:].bitcast(FP8X4), scales=z_bytes[:, CHUNK:], in_=z_second_grouped[:])
+
+        w3_codes = keep.tile([P, N], U32, tag="y3", align_bytes=64)
+        w3_bytes = keep.tile([P, N], U8, align_bytes=64)
+        nc.vector.tensor_copy(
+            out=w3_codes[:].rearrange("p (t m) -> p m t", t=PACK),
+            in_=w3_table[:].bitcast(U32).rearrange("p (m t) -> p m t", t=PACK),
+        )
+        nc.vector.tensor_copy(
+            out=w3_bytes[:].rearrange("p (t m) -> p m t", t=PACK),
+            in_=w3_scale_table[:].rearrange("p (m t) -> p m t", t=PACK),
+        )
+        second_layer(3, 0, "h00")
+        for t in range(PACK):
+            second_layer(t, 1, "h%d1" % t)
+
+        out_rows = out_0.rearrange("(p t) v -> p t v", t=PACK)
+        out_words = out_1[0].rearrange("p n r -> p (n r)").bitcast(I32)
+        out_codes = keep.tile([P, V], U32, align_bytes=64)
+        out_bytes = keep.tile([P, V], U8, align_bytes=64)
+        z2_codes = keep.tile([P, V], U32, align_bytes=64)
+        z2_bytes = keep.tile([P, V], U8, align_bytes=64)
+        chunks = V // CHUNK
+
+        def grouped_cols(tile, first, count):
+            return tile[:, PACK * first : PACK * (first + count)]
+
+        def quantize(codes, scales, first, count, grouped):
+            cols = slice(first, first + count)
+            nc.vector.quantize_mx(out=codes[:, cols].bitcast(FP8X4), scales=scales[:, cols], in_=grouped)
+
+        def last_layer(first):
+            cols = slice(first, first + HALF)
+            bank = psum.tile([P, PACK, HALF], F32, tag="bank")
+            for t in range(PACK):
+                mx_product(bank[:, t, :], w3_codes, w3_bytes, t, z2_codes[:, cols], z2_bytes[:, cols])
+            return bank
+
+        z2_even = keep.tile([P, PACK * CHUNK], BF16, tag="z2_even", align_bytes=64)
+        z2_shared = keep.tile([P, 6 * CHUNK], BF16, tag="h31", align_bytes=64)
+        for c in range(chunks):
+            c0 = c * CHUNK
+            cols = slice(c0, c0 + CHUNK)
+            if c == 0:
+                z2 = z2_even[:]
+                z2_grouped = z2_shared[:, 2 * CHUNK :]
+            else:
+                if c == 1:
+                    z2 = z2_shared[:, : PACK * CHUNK]
+                else:
+                    z2 = keep.tile([P, PACK * CHUNK], BF16, name="z2", tag="z2_even" if c == 2 else "h31", align_bytes=64)[:]
+                z2_grouped = keep.tile([P, PACK * CHUNK], BF16, name="z2_grouped%d" % c, align_bytes=64)[:]
+            for t in range(PACK):
+                read_page(z2, t, rd2_list, c0)
+            if c < chunks - 1:
+                interleave(nc.scalar.copy if c in SCALAR_CHUNKS else nc.vector.tensor_copy, z2_grouped, z2.rearrange("p (t n) -> p t n", t=PACK))
+                quantize(z2_codes, z2_bytes, c0, CHUNK, z2_grouped)
+                result = keep.tile([P, PACK, CHUNK], F32, name="result%d" % c, align_bytes=64)
+                result_grouped = keep.tile([P, CHUNK * PACK], BF16, name="result_grouped%d" % c, align_bytes=64)
+                for h0 in range(0, CHUNK, HALF):
+                    bank = last_layer(c0 + h0)
+                    nc.scalar.copy(out=result[:, :, h0 : h0 + HALF], in_=bank[:])
+                    nc.scalar.copy(
+                        out=grouped_cols(result_grouped, h0, HALF).rearrange("p (n t) -> p n t", t=PACK),
+                        in_=bank[:].rearrange("p t n -> p n t"),
+                    )
+                nc.sync.dma_start(out=out_rows[:, :, cols], in_=result[:])
+                quantize(out_codes, out_bytes, c0, CHUNK, result_grouped[:])
+                nc.sync.dma_start(out=out_words[:, cols], in_=out_codes[:, cols].bitcast(I32))
+            else:
+                planes = z2.rearrange("p (t n) -> p t n", t=PACK)
+                for h0 in range(0, CHUNK, HALF):
+                    interleave(nc.vector.tensor_copy, grouped_cols(z2_grouped, h0, HALF), planes[:, :, h0 : h0 + HALF])
+                for h0 in range(0, CHUNK, HALF):
+                    quantize(z2_codes, z2_bytes, c0 + h0, HALF, grouped_cols(z2_grouped, h0, HALF))
+                result_grouped = keep.tile([P, CHUNK * PACK], BF16, name="result_grouped%d" % c, align_bytes=64)
+                for h0 in range(0, CHUNK, HALF):
+                    bank = last_layer(c0 + h0)
+                    result = keep.tile([P, PACK, HALF], F32, name="result_half%d" % h0, align_bytes=64)
+                    nc.scalar.copy(out=result[:], in_=bank[:])
+                    nc.sync.dma_start(out=out_rows[:, :, c0 + h0 : c0 + h0 + HALF], in_=result[:])
+                    interleave(nc.vector.tensor_copy, grouped_cols(result_grouped, h0, HALF), result[:])
+                quantize(out_codes, out_bytes, c0, CHUNK, result_grouped[:])
+                nc.sync.dma_start(out=out_words[:, cols], in_=out_codes[:, cols].bitcast(I32))
+        for q in range(4):
+            queue = nc.sync if q < 2 else nc.scalar
+            queue.dma_start(
+                out=out_2[0][4 * q : 4 * q + 4, :].bitcast(I32),
+                in_=out_bytes[32 * q : 32 * q + 4, :].bitcast(I32),
+            )

@@ -92,10 +92,10 @@ def tile_picked_pagerd_relu_po_kernel(
         nc.sync.dma_start(slot_list[:], slot)
         nc.sync.dma_start(out=page[0][:], in_=mem_rows[0])
         nc.sync.dma_start(out=page[1][:], in_=mem_rows[1])
+        nc.sync.dma_start(out=w2_raw[:], in_=w2.rearrange("(p j) c -> p j c", j=PACK))
         nc.sync.dma_start(rd_list[:], rd)
         nc.sync.dma_start(out=page[2][:], in_=mem_rows[2])
         nc.sync.dma_start(out=page[3][:], in_=mem_rows[3])
-        nc.sync.dma_start(out=w2_raw[:], in_=w2.rearrange("(p j) c -> p j c", j=PACK))
         nc.sync.dma_start(put_list[:], put)
         nc.sync.dma_start(out=w3_table[:], in_=w3_words[0].rearrange("p n r -> p (n r)").bitcast(I32))
         load_scale_rows(nc, w3_scale_table, w3_scales[0])

from contextlib import ExitStack

import concourse.mybir as mybir

K, T, S, V, N, U, H = 512, 2048, 512, 1024, 512, 1024, 512
FLOPS = 2 * K * H * S + 2 * H * H * S + 2 * H * N * V

F32 = mybir.dt.float32
BF16 = mybir.dt.bfloat16
I32 = mybir.dt.int32
U32 = mybir.dt.uint32
U16 = mybir.dt.uint16
U8 = mybir.dt.uint8
FP8X4 = mybir.dt.float8_e4m3fn_x4
RELU = mybir.ActivationFunctionType.Relu

P = 128
PACK = 4
CHUNK = 256
HALF = 128
W1_VECTOR_SHARE = 80
SCALAR_CHUNKS = (0,)


def entries(lists, first, count):
    return lists[:, first // 16 : (first + count) // 16]


def deal_weight(engine_copy, grouped, raw, m0, m1):
    engine_copy(
        out=grouped[:].rearrange("p t m j -> p m j t")[:, m0:m1],
        in_=raw[:].rearrange("p j (m t) -> p m j t", t=PACK)[:, m0:m1],
    )


def interleave(engine_copy, out, in_):
    engine_copy(
        out=out.rearrange("p (c i t) -> p c t i", i=4, t=PACK),
        in_=in_.rearrange("p t (c i) -> p c t i", i=4),
    )


def load_scale_rows(nc, plane, rows):
    for q in range(4):
        nc.sync.dma_start(
            out=plane[32 * q : 32 * q + 4, :].bitcast(I32),
            in_=rows[4 * q : 4 * q + 4, :].bitcast(I32),
        )


def tile_picked_pagerd_relu_po_kernel(
    tc, x_words, x_scales, w1, mem, w2, w3_words, w3_scales, offs, slot, rd, put, rd2, out_0, out_1, out_2
):
    nc = tc.nc
    with ExitStack() as ctx:
        keep = ctx.enter_context(tc.tile_pool(name="keep", bufs=1))
        psum = ctx.enter_context(tc.psum_pool(name="psum", bufs=8))

        def mx_product(out, w_codes, w_scales, t, codes, scales):
            cols = slice(t * P, (t + 1) * P)
            nc.tensor.matmul_mx(
                out=out,
                lhsT=w_codes[:, cols].bitcast(FP8X4),
                lhsT_scale=w_scales[:, cols],
                rhs=codes.bitcast(FP8X4),
                rhs_scale=scales,
                start=True,
                stop=True,
            )

        offs_list = keep.tile([P, S // 16], U16)
        slot_list = keep.tile([P, S // 16], U16)
        rd_list = keep.tile([P, S // 16], U16)
        put_list = keep.tile([P, S // 16], U16)
        rd2_list = keep.tile([P, V // 16], U16)
        x_table = keep.tile([P, T], I32, align_bytes=64)
        x_scale_table = keep.tile([P, T], U8, align_bytes=64)
        w1_raw = keep.tile([P, PACK, H], F32)
        w2_raw = keep.tile([P, PACK, H], F32)
        w3_table = keep.tile([P, N], I32, align_bytes=64)
        w3_scale_table = keep.tile([P, N], U8, align_bytes=64)
        page = [keep.tile([P, U], F32, name="page%d" % t, align_bytes=64) for t in range(PACK)]

        nc.vector.memset(x_scale_table[:].bitcast(I32), 0)
        nc.vector.memset(w3_scale_table[:].bitcast(I32), 0)

        mem_rows = mem.rearrange("(p t) u -> t p u", t=PACK)
        nc.sync.dma_start(out=w1_raw[:], in_=w1.rearrange("(p j) c -> p j c", j=PACK))
        load_scale_rows(nc, x_scale_table, x_scales[0])
        nc.sync.dma_start(offs_list[:], offs)
        nc.sync.dma_start(out=x_table[:], in_=x_words[0].rearrange("p n r -> p (n r)").bitcast(I32))
        nc.sync.dma_start(slot_list[:], slot)
        nc.sync.dma_start(out=page[0][:], in_=mem_rows[0])
        nc.sync.dma_start(out=page[1][:], in_=mem_rows[1])
        nc.sync.dma_start(out=w2_raw[:], in_=w2.rearrange("(p j) c -> p j c", j=PACK))
        nc.sync.dma_start(rd_list[:], rd)
        nc.sync.dma_start(out=page[2][:], in_=mem_rows[2])
        nc.sync.dma_start(out=page[3][:], in_=mem_rows[3])
        nc.sync.dma_start(put_list[:], put)
        nc.sync.dma_start(out=w3_table[:], in_=w3_words[0].rearrange("p n r -> p (n r)").bitcast(I32))
        load_scale_rows(nc, w3_scale_table, w3_scales[0])
        nc.sync.dma_start(rd2_list[:], rd2)

        w1_grouped = keep.tile([P, PACK, P, PACK], BF16, align_bytes=64)
        deal_weight(nc.vector.tensor_copy, w1_grouped, w1_raw, 0, W1_VECTOR_SHARE)
        deal_weight(nc.scalar.copy, w1_grouped, w1_raw, W1_VECTOR_SHARE, P)
        x_bytes = keep.tile([P, S], U8, align_bytes=64)
        nc.vector.tensor_copy(out=x_bytes[:], in_=x_scale_table[:].indirect(offs_list[:]))
        w1_codes = keep.tile([P, H], U32, align_bytes=64)
        w1_bytes = keep.tile([P, H], U8, align_bytes=64)
        nc.vector.quantize_mx(
            out=w1_codes[:].bitcast(FP8X4),
            scales=w1_bytes[:],
            in_=w1_grouped[:].rearrange("p t m j -> p (t m j)"),
        )

        x_codes = keep.tile([P, S], U32, align_bytes=64)
        for c0 in range(0, S, CHUNK):
            nc.vector.tensor_copy(
                out=x_codes[:, c0 : c0 + CHUNK],
                in_=x_table[:].bitcast(U32).indirect(entries(offs_list, c0, CHUNK)),
            )

        y_sb = [keep.tile([P, S], F32, name="y%d" % t, tag="y%d" % t, align_bytes=64) for t in range(PACK)]
        for t in range(PACK):
            width = CHUNK if t == 0 else S
            for c0 in range(0, S, width):
                cols = slice(c0, c0 + width)
                bank = psum.tile([P, S], F32, tag="bank")
                mx_product(bank[:, :width], w1_codes, w1_bytes, t, x_codes[:, cols], x_bytes[:, cols])
                nc.scalar.copy(out=y_sb[t][:, cols], in_=bank[:, :width])
                nc.vector.tensor_copy(out=page[t][:].indirect(entries(slot_list, c0, width)), in_=y_sb[t][:, cols])

        w2_grouped = keep.tile([P, PACK, P, PACK], BF16, align_bytes=64)
        deal_weight(nc.scalar.copy, w2_grouped, w2_raw, 0, P)
        w2_codes = keep.tile([P, H], U32, align_bytes=64)
        w2_bytes = keep.tile([P, H], U8, align_bytes=64)

        def read_page(out, t, lists, c0):
            nc.vector.tensor_copy(
                out=out[:, t * CHUNK : (t + 1) * CHUNK],
                in_=page[t][:].indirect(entries(lists, c0, CHUNK)),
            )

        z_first = keep.tile([P, PACK * CHUNK], BF16, align_bytes=64)
        z_shared = keep.tile([P, 6 * CHUNK], BF16, tag="y3", align_bytes=64)
        z_second = z_shared[:, : PACK * CHUNK]
        z_first_grouped = z_shared[:, 2 * CHUNK :]
        z_codes = keep.tile([P, S], U32, align_bytes=64)
        z_bytes = keep.tile([P, S], U8, align_bytes=64)

        def second_layer(t, c, tag):
            cols = slice(c * CHUNK, (c + 1) * CHUNK)
            bank = psum.tile([P, S], F32, tag="bank")
            mx_product(bank[:, :CHUNK], w2_codes, w2_bytes, t, z_codes[:, cols], z_bytes[:, cols])
            h = keep.tile([P, CHUNK], F32, name="h", tag=tag, align_bytes=64)
            nc.scalar.activation(out=h[:], in_=bank[:, :CHUNK], func=RELU)
            nc.vector.tensor_copy(out=page[t][:].indirect(entries(put_list, c * CHUNK, CHUNK)), in_=h[:])

        for t in range(PACK):
            read_page(z_first, t, rd_list, 0)
        interleave(nc.scalar.copy, z_first_grouped, z_first[:].rearrange("p (t n) -> p t n", t=PACK))
        for t in range(2):
            read_page(z_second, t, rd_list, CHUNK)
        nc.vector.quantize_mx(
            out=w2_codes[:].bitcast(FP8X4),
            scales=w2_bytes[:],
            in_=w2_grouped[:].rearrange("p t m j -> p (t m j)"),
        )
        nc.vector.quantize_mx(out=z_codes[:, :CHUNK].bitcast(FP8X4), scales=z_bytes[:, :CHUNK], in_=z_first_grouped)
        for t in range(2, PACK):
            read_page(z_second, t, rd_list, CHUNK)
        second_layer(0, 0, "h00")
        z_second_grouped = keep.tile([P, PACK * CHUNK], BF16, tag="h00", align_bytes=64)
        interleave(nc.scalar.copy, z_second_grouped[:], z_second.rearrange("p (t n) -> p t n", t=PACK))
        second_layer(1, 0, "h10")
        second_layer(2, 0, "h20")
        nc.vector.quantize_mx(out=z_codes[:, CHUNK:].bitcast(FP8X4), scales=z_bytes[:, CHUNK:], in_=z_second_grouped[:])

        w3_codes = keep.tile([P, N], U32, tag="y3", align_bytes=64)
        w3_bytes = keep.tile([P, N], U8, align_bytes=64)
        nc.vector.tensor_copy(
            out=w3_codes[:].rearrange("p (t m) -> p m t", t=PACK),
            in_=w3_table[:].bitcast(U32).rearrange("p (m t) -> p m t", t=PACK),
        )
        nc.vector.tensor_copy(
            out=w3_bytes[:].rearrange("p (t m) -> p m t", t=PACK),
            in_=w3_scale_table[:].rearrange("p (m t) -> p m t", t=PACK),
        )
        second_layer(3, 0, "h00")
        for t in range(PACK):
            second_layer(t, 1, "h%d1" % t)

        out_rows = out_0.rearrange("(p t) v -> p t v", t=PACK)
        out_words = out_1[0].rearrange("p n r -> p (n r)").bitcast(I32)
        out_codes = keep.tile([P, V], U32, align_bytes=64)
        out_bytes = keep.tile([P, V], U8, align_bytes=64)
        z2_codes = keep.tile([P, V], U32, align_bytes=64)
        z2_bytes = keep.tile([P, V], U8, align_bytes=64)
        chunks = V // CHUNK

        def grouped_cols(tile, first, count):
            return tile[:, PACK * first : PACK * (first + count)]

        def quantize(codes, scales, first, count, grouped):
            cols = slice(first, first + count)
            nc.vector.quantize_mx(out=codes[:, cols].bitcast(FP8X4), scales=scales[:, cols], in_=grouped)

        def last_layer(first):
            cols = slice(first, first + HALF)
            bank = psum.tile([P, PACK, HALF], F32, tag="bank")
            for t in range(PACK):
                mx_product(bank[:, t, :], w3_codes, w3_bytes, t, z2_codes[:, cols], z2_bytes[:, cols])
            return bank

        z2_even = keep.tile([P, PACK * CHUNK], BF16, tag="z2_even", align_bytes=64)
        z2_shared = keep.tile([P, 6 * CHUNK], BF16, tag="h31", align_bytes=64)
        for c in range(chunks):
            c0 = c * CHUNK
            cols = slice(c0, c0 + CHUNK)
            if c == 0:
                z2 = z2_even[:]
                z2_grouped = z2_shared[:, 2 * CHUNK :]
            else:
                if c == 1:
                    z2 = z2_shared[:, : PACK * CHUNK]
                else:
                    z2 = keep.tile([P, PACK * CHUNK], BF16, name="z2", tag="z2_even" if c == 2 else "h31", align_bytes=64)[:]
                z2_grouped = keep.tile([P, PACK * CHUNK], BF16, name="z2_grouped%d" % c, align_bytes=64)[:]
            for t in range(PACK):
                read_page(z2, t, rd2_list, c0)
            if c < chunks - 1:
                interleave(nc.scalar.copy if c in SCALAR_CHUNKS else nc.vector.tensor_copy, z2_grouped, z2.rearrange("p (t n) -> p t n", t=PACK))
                quantize(z2_codes, z2_bytes, c0, CHUNK, z2_grouped)
                result = keep.tile([P, PACK, CHUNK], F32, name="result%d" % c, align_bytes=64)
                result_grouped = keep.tile([P, CHUNK * PACK], BF16, name="result_grouped%d" % c, align_bytes=64)
                for h0 in range(0, CHUNK, HALF):
                    bank = last_layer(c0 + h0)
                    nc.scalar.copy(out=result[:, :, h0 : h0 + HALF], in_=bank[:])
                    nc.scalar.copy(
                        out=grouped_cols(result_grouped, h0, HALF).rearrange("p (n t) -> p n t", t=PACK),
                        in_=bank[:].rearrange("p t n -> p n t"),
                    )
                nc.sync.dma_start(out=out_rows[:, :, cols], in_=result[:])
                quantize(out_codes, out_bytes, c0, CHUNK, result_grouped[:])
                nc.sync.dma_start(out=out_words[:, cols], in_=out_codes[:, cols].bitcast(I32))
            else:
                planes = z2.rearrange("p (t n) -> p t n", t=PACK)
                for h0 in range(0, CHUNK, HALF):
                    interleave(nc.vector.tensor_copy, grouped_cols(z2_grouped, h0, HALF), planes[:, :, h0 : h0 + HALF])
                for h0 in range(0, CHUNK, HALF):
                    quantize(z2_codes, z2_bytes, c0 + h0, HALF, grouped_cols(z2_grouped, h0, HALF))
                result_grouped = keep.tile([P, CHUNK * PACK], BF16, name="result_grouped%d" % c, align_bytes=64)
                for h0 in range(0, CHUNK, HALF):
                    bank = last_layer(c0 + h0)
                    result = keep.tile([P, PACK, HALF], F32, name="result_half%d" % h0, align_bytes=64)
                    nc.scalar.copy(out=result[:], in_=bank[:])
                    nc.sync.dma_start(out=out_rows[:, :, c0 + h0 : c0 + h0 + HALF], in_=result[:])
                    interleave(nc.vector.tensor_copy, grouped_cols(result_grouped, h0, HALF), result[:])
                quantize(out_codes, out_bytes, c0, CHUNK, result_grouped[:])
                nc.sync.dma_start(out=out_words[:, cols], in_=out_codes[:, cols].bitcast(I32))
        for q in range(4):
            queue = nc.sync if q < 2 else nc.scalar
            queue.dma_start(
                out=out_2[0][4 * q : 4 * q + 4, :].bitcast(I32),
                in_=out_bytes[32 * q : 32 * q + 4, :].bitcast(I32),
            )
